import numpy as np, ml_dtypes
CORES = [3,7,11,15,131,135,139,143]
N = 8
NP, TK = 4, 128
def setup_inputs(rng):
    return {"x": rng.standard_normal((N, 128, TK), dtype=np.float32).astype(ml_dtypes.bfloat16), "w1": (rng.standard_normal((N, 128, 128), dtype=np.float32) / 8).astype(ml_dtypes.bfloat16), "w2": (rng.standard_normal((N, 128, NP * 128), dtype=np.float32) / 8).astype(ml_dtypes.bfloat16)}
def setup_inputs_big(rng):
    d = setup_inputs(rng)
    for k in ("x", "w1", "w2"): d[k] = (d[k].astype(np.float32) * 1024.0).astype(d[k].dtype)
    return d
def setup_inputs_small(rng):
    d = setup_inputs(rng)
    for k in ("x", "w1", "w2"): d[k] = (d[k].astype(np.float32) * (1 / 1024.0)).astype(d[k].dtype)
    return d
def setup_inputs_apart(rng):
    d = setup_inputs(rng)
    f = (10.0 ** rng.permutation(np.linspace(-1.5, 1.5, N))).astype(np.float32).reshape(N, 1, 1)
    for k in ("x", "w1", "w2"): d[k] = (d[k].astype(np.float32) * f).astype(d[k].dtype)
    return d
def reference(x, w1, w2):
    X, W1, W2 = x.astype(np.float64), w1.astype(np.float64), w2.astype(np.float64)
    h = [np.maximum(W1[p].T @ X[p], 0.0) for p in range(NP)]
    y = np.full((N, 128, TK), np.nan)
    for q in range(NP, N):
        y[q] = sum(W2[q][:, 128 * p:128 * p + 128].T @ h[p] for p in range(NP))
    return {"y": y.astype(ml_dtypes.bfloat16 if x.dtype != np.float64 else np.float64)}

@@ -1,0 +1,74 @@
+from concourse.bass import DstId, RemoteDMATransfer
+from concourse.mybir import AluOpType
+
+NP, TK = 4, 128
+
+SCRATCH = {
+    "xs": ("sbuf", [128, TK], "bfloat16"),
+    "w1s": ("sbuf", [128, 128], "bfloat16"),
+    "zero": ("sbuf", [128, TK], "float32"),
+    "hs": ("sbuf", [128, TK], "bfloat16"),
+    "w2s": ("sbuf", [128, NP * 128], "bfloat16"),
+    "land": ("sbuf", [128, NP * TK], "bfloat16"),
+    "ys": ("sbuf", [128, TK], "bfloat16"),
+    "acc": ("psum", [128, TK], "float32"),
+}
+SEMAPHORES = ["ld", "zs", "mm", "hr", "sent", "cp", "st"] + ["arr%d" % p for p in range(NP)]
+
+
+def _count(mask):
+    return bin(mask).count("1")
+
+
+def rank_program(g, core, T, topo):
+    rank = T.rank_of(core)
+    if rank is None:
+        return
+    S = T.sem
+    if rank < NP:
+        p = rank
+        g.sync.dma_start(T.xs[:], T.x[:]).then_inc(S.ld, 16)
+        g.scalar.dma_start(T.w1s[:], T.w1[:]).then_inc(S.ld, 16)
+        g.vector.memset(T.zero[:], 0.0).then_inc(S.zs, 1)
+
+        g.tensor.wait_ge(S.ld, 32)
+        g.tensor.matmul(T.acc[:], T.w1s[:], T.xs[:], True, True).then_inc(S.mm, 1)
+
+        g.vector.wait_ge(S.zs, 1)
+        g.vector.wait_ge(S.mm, 1)
+        g.vector.tensor_tensor(T.hs[:], T.acc[:], T.zero[:], AluOpType.max).then_inc(S.hr, 1)
+
+        dsts = [T.cores[NP + (p + k) % NP] for k in range(NP)]
+        mask = topo.mask(core, dsts[0])
+        for d in dsts:
+            mask &= topo.mask(core, d)
+        ids = []
+        for d in dsts:
+            rid, pid = topo.addr(d, core)
+            ids.append(DstId(rid=rid, pnc=pid))
+        blk = T.land[:, p * TK:(p + 1) * TK]
+        g.wait_ge(S.hr, 1)
+        g.remote_dma_fused(
+            [RemoteDMATransfer(dst_ids=ids, dma_engine_mask=mask, remote_sem=S["arr%d" % p],
+                               srcs=[T.hs[:]], dsts=[blk for _ in dsts], alu_op=0)],
+            local_sem=S.sent)
+        g.wait_ge(S.sent, _count(mask))
+    else:
+        j = rank - NP
+        g.scalar.dma_start(T.w2s[:], T.w2[:]).then_inc(S.ld, 16)
+        g.tensor.wait_ge(S.ld, 16)
+        for k in range(NP):
+            p = (j - k) % NP
+            src = T.cores[p]
+            m = topo.mask(src, T.cores[NP])
+            for d in T.cores[NP:]:
+                m &= topo.mask(src, d)
+            g.tensor.wait_ge(S["arr%d" % p], _count(m))
+            mmi = g.tensor.matmul(T.acc[:], T.w2s[:, p * 128:(p + 1) * 128], T.land[:, p * TK:(p + 1) * TK],
+                                  k == 0, k == NP - 1)
+        mmi.then_inc(S.mm, 1)
+        g.vector.wait_ge(S.mm, 1)
+        g.vector.tensor_copy(T.ys[:], T.acc[:]).then_inc(S.cp, 1)
+        g.sync.wait_ge(S.cp, 1)
+        g.sync.dma_start(T.y[:], T.ys[:]).then_inc(S.st, 16)
+        g.sync.wait_ge(S.st, 16)

@@ -16,6 +16,17 @@ SCRATCH = {
 SEMAPHORES = ["ld", "zs", "mm", "hr", "sent", "cp", "st"] + ["arr%d" % p for p in range(NP)]
 
 
+def _way(topo, a, b):
+    return (0 if topo.same_plane(a, b) else 2) + (0 if topo.die(a) == topo.die(b) else 1)
+
+
+def _mask(topo, src, dsts):
+    m = topo.mask(src, dsts[0])
+    for d in dsts:
+        m &= topo.mask(src, d)
+    return m
+
+
 def _count(mask):
     return bin(mask).count("1")
 
@@ -25,6 +36,7 @@ def rank_program(g, core, T, topo):
     if rank is None:
         return
     S = T.sem
+    P, Q = T.cores[:NP], T.cores[NP:]
     if rank < NP:
         p = rank
         g.sync.dma_start(T.xs[:], T.x[:]).then_inc(S.ld, 16)
@@ -38,32 +50,28 @@ def rank_program(g, core, T, topo):
         g.vector.wait_ge(S.mm, 1)
         g.vector.tensor_tensor(T.hs[:], T.acc[:], T.zero[:], AluOpType.max).then_inc(S.hr, 1)
 
-        dsts = [T.cores[NP + (p + k) % NP] for k in range(NP)]
-        mask = topo.mask(core, dsts[0])
-        for d in dsts:
-            mask &= topo.mask(core, d)
-        ids = []
-        for d in dsts:
-            rid, pid = topo.addr(d, core)
-            ids.append(DstId(rid=rid, pnc=pid))
+        dsts = sorted(Q, key=lambda q: -_way(topo, core, q))
+        mask = _mask(topo, core, Q)
         blk = T.land[:, p * TK:(p + 1) * TK]
+        groups = [[d for d in dsts if not topo.same_plane(core, d)], [d for d in dsts if topo.same_plane(core, d)]]
         g.wait_ge(S.hr, 1)
-        g.remote_dma_fused(
-            [RemoteDMATransfer(dst_ids=ids, dma_engine_mask=mask, remote_sem=S["arr%d" % p],
-                               srcs=[T.hs[:]], dsts=[blk for _ in dsts], alu_op=0)],
-            local_sem=S.sent)
-        g.wait_ge(S.sent, _count(mask))
+        for grp in groups:
+            ids = []
+            for d in grp:
+                rid, pid = topo.addr(d, core)
+                ids.append(DstId(rid=rid, pnc=pid))
+            g.remote_dma_fused(
+                [RemoteDMATransfer(dst_ids=ids, dma_engine_mask=mask, remote_sem=S["arr%d" % p],
+                                   srcs=[T.hs[:]], dsts=[blk for _ in grp], alu_op=0)],
+                local_sem=S.sent)
+        g.wait_ge(S.sent, len(groups) * _count(mask))
     else:
-        j = rank - NP
         g.scalar.dma_start(T.w2s[:], T.w2[:]).then_inc(S.ld, 16)
         g.tensor.wait_ge(S.ld, 16)
-        for k in range(NP):
-            p = (j - k) % NP
-            src = T.cores[p]
-            m = topo.mask(src, T.cores[NP])
-            for d in T.cores[NP:]:
-                m &= topo.mask(src, d)
-            g.tensor.wait_ge(S["arr%d" % p], _count(m))
+        srcs = sorted(P, key=lambda s: -_way(topo, s, core))
+        for k, s in enumerate(srcs):
+            p = T.rank_of(s)
+            g.tensor.wait_ge(S["arr%d" % p], _count(_mask(topo, s, Q)))
             mmi = g.tensor.matmul(T.acc[:], T.w2s[:, p * 128:(p + 1) * 128], T.land[:, p * TK:(p + 1) * TK],
                                   k == 0, k == NP - 1)
         mmi.then_inc(S.mm, 1)

@@ -2,22 +2,29 @@ from concourse.bass import DstId, RemoteDMATransfer
 from concourse.mybir import AluOpType
 
 NP, TK = 4, 128
+HEAD = 32
+XW = TK + 128
 
 SCRATCH = {
-    "xs": ("sbuf", [128, TK], "bfloat16"),
-    "w1s": ("sbuf", [128, 128], "bfloat16"),
+    "xw": ("sbuf", [128, XW], "bfloat16"),
     "zero": ("sbuf", [128, TK], "float32"),
     "hs": ("sbuf", [128, TK], "bfloat16"),
     "w2s": ("sbuf", [128, NP * 128], "bfloat16"),
+    "raw": ("sbuf", [128, XW], "bfloat16"),
     "land": ("sbuf", [128, NP * TK], "bfloat16"),
     "ys": ("sbuf", [128, TK], "bfloat16"),
-    "acc": ("psum", [128, TK], "float32"),
+    "acc": ("psum", [128, 512], "float32"),
+    "acch": ("psum", [128, 512], "float32"),
 }
-SEMAPHORES = ["ld", "zs", "mm", "hr", "sent", "cp", "st"] + ["arr%d" % p for p in range(NP)]
+SEMAPHORES = ["ldh", "ld", "zs", "hm", "mm", "hr", "sent", "cp", "st", "rawarr"] + ["arr%d" % p for p in range(NP)]
 
 
 def _way(topo, a, b):
     return (0 if topo.same_plane(a, b) else 2) + (0 if topo.die(a) == topo.die(b) else 1)
+
+
+def _gets_inputs(topo, p, q):
+    return topo.same_plane(p, q) and topo.die(p) != topo.die(q)
 
 
 def _mask(topo, src, dsts):
@@ -31,52 +38,75 @@ def _count(mask):
     return bin(mask).count("1")
 
 
+def _send(g, topo, core, mask, dsts, src, dst, remote_sem, local_sem):
+    ids = []
+    for d in dsts:
+        rid, pid = topo.addr(d, core)
+        ids.append(DstId(rid=rid, pnc=pid))
+    g.remote_dma_fused(
+        [RemoteDMATransfer(dst_ids=ids, dma_engine_mask=mask, remote_sem=remote_sem,
+                           srcs=[src], dsts=[dst for _ in dsts], alu_op=0)],
+        local_sem=local_sem)
+
+
+def _layer1(g, T, S, buf):
+    g.tensor.matmul(T.acch[:, 0:TK], buf[:, TK:XW], buf[:, 0:TK], True, True).then_inc(S.hm, 1)
+    g.vector.wait_ge(S.zs, 1)
+    g.vector.wait_ge(S.hm, 1)
+    g.vector.tensor_tensor(T.hs[:], T.acch[:, 0:TK], T.zero[:], AluOpType.max).then_inc(S.hr, 1)
+
+
 def rank_program(g, core, T, topo):
     rank = T.rank_of(core)
     if rank is None:
         return
     S = T.sem
     P, Q = T.cores[:NP], T.cores[NP:]
+    g.vector.memset(T.zero[:], 0.0).then_inc(S.zs, 1)
     if rank < NP:
         p = rank
-        g.sync.dma_start(T.xs[:], T.x[:]).then_inc(S.ld, 16)
-        g.scalar.dma_start(T.w1s[:], T.w1[:]).then_inc(S.ld, 16)
-        g.vector.memset(T.zero[:], 0.0).then_inc(S.zs, 1)
+        g.sync.dma_start(T.xw[:, 0:HEAD], T.x[:, 0:HEAD]).then_inc(S.ldh, 16)
+        g.scalar.dma_start(T.xw[:, TK:XW], T.w1[:]).then_inc(S.ld, 16)
+        g.sync.dma_start(T.xw[:, HEAD:TK], T.x[:, HEAD:TK]).then_inc(S.ld, 16)
 
-        g.tensor.wait_ge(S.ld, 32)
-        g.tensor.matmul(T.acc[:], T.w1s[:], T.xs[:], True, True).then_inc(S.mm, 1)
-
-        g.vector.wait_ge(S.zs, 1)
-        g.vector.wait_ge(S.mm, 1)
-        g.vector.tensor_tensor(T.hs[:], T.acc[:], T.zero[:], AluOpType.max).then_inc(S.hr, 1)
-
-        dsts = sorted(Q, key=lambda q: -_way(topo, core, q))
         mask = _mask(topo, core, Q)
-        blk = T.land[:, p * TK:(p + 1) * TK]
-        groups = [[d for d in dsts if not topo.same_plane(core, d)], [d for d in dsts if topo.same_plane(core, d)]]
+        first = [q for q in Q if _gets_inputs(topo, core, q)]
+        rest = sorted([q for q in Q if q not in first], key=lambda q: -_way(topo, core, q))
+
+        g.wait_ge(S.ldh, 16)
+        _send(g, topo, core, mask, first, T.xw[:, 0:HEAD], T.raw[:, 0:HEAD], S.rawarr, S.sent)
+        g.wait_ge(S.ld, 32)
+        _send(g, topo, core, mask, first, T.xw[:, HEAD:XW], T.raw[:, HEAD:XW], S.rawarr, S.sent)
+
+        g.tensor.wait_ge(S.ldh, 16)
+        g.tensor.wait_ge(S.ld, 32)
+        _layer1(g, T, S, T.xw)
+
         g.wait_ge(S.hr, 1)
-        for grp in groups:
-            ids = []
-            for d in grp:
-                rid, pid = topo.addr(d, core)
-                ids.append(DstId(rid=rid, pnc=pid))
-            g.remote_dma_fused(
-                [RemoteDMATransfer(dst_ids=ids, dma_engine_mask=mask, remote_sem=S["arr%d" % p],
-                                   srcs=[T.hs[:]], dsts=[blk for _ in grp], alu_op=0)],
-                local_sem=S.sent)
-        g.wait_ge(S.sent, len(groups) * _count(mask))
+        _send(g, topo, core, mask, rest, T.hs[:], T.land[:, p * TK:(p + 1) * TK], S["arr%d" % p], S.sent)
+        g.wait_ge(S.sent, 3 * _count(mask))
     else:
         g.scalar.dma_start(T.w2s[:], T.w2[:]).then_inc(S.ld, 16)
+        own = [s for s in P if _gets_inputs(topo, s, core)][0]
+        rest = sorted([s for s in P if s != own], key=lambda s: -_way(topo, s, core))
+
+        g.tensor.wait_ge(S.rawarr, 2 * _count(_mask(topo, own, Q)))
+        _layer1(g, T, S, T.raw)
+
         g.tensor.wait_ge(S.ld, 16)
-        srcs = sorted(P, key=lambda s: -_way(topo, s, core))
-        for k, s in enumerate(srcs):
+        turns = [rest[0], own] + rest[1:]
+        for k, s in enumerate(turns):
             p = T.rank_of(s)
-            g.tensor.wait_ge(S["arr%d" % p], _count(_mask(topo, s, Q)))
-            mmi = g.tensor.matmul(T.acc[:], T.w2s[:, p * 128:(p + 1) * 128], T.land[:, p * TK:(p + 1) * TK],
-                                  k == 0, k == NP - 1)
+            if s == own:
+                g.tensor.wait_ge(S.hr, 1)
+                h = T.hs[:]
+            else:
+                g.tensor.wait_ge(S["arr%d" % p], _count(_mask(topo, s, Q)))
+                h = T.land[:, p * TK:(p + 1) * TK]
+            mmi = g.tensor.matmul(T.acc[:, 0:TK], T.w2s[:, p * 128:(p + 1) * 128], h, k == 0, k == NP - 1)
         mmi.then_inc(S.mm, 1)
         g.vector.wait_ge(S.mm, 1)
-        g.vector.tensor_copy(T.ys[:], T.acc[:]).then_inc(S.cp, 1)
+        g.vector.tensor_copy(T.ys[:], T.acc[:, 0:TK]).then_inc(S.cp, 1)
         g.sync.wait_ge(S.cp, 1)
         g.sync.dma_start(T.y[:], T.ys[:]).then_inc(S.st, 16)
         g.sync.wait_ge(S.st, 16)

from concourse.bass import DstId, RemoteDMATransfer
from concourse.mybir import AluOpType

NP, TK = 4, 128
HEAD = 32
XW = TK + 128

SCRATCH = {
    "xw": ("sbuf", [128, XW], "bfloat16"),
    "zero": ("sbuf", [128, TK], "float32"),
    "hs": ("sbuf", [128, TK], "bfloat16"),
    "w2s": ("sbuf", [128, NP * 128], "bfloat16"),
    "raw": ("sbuf", [128, XW], "bfloat16"),
    "land": ("sbuf", [128, NP * TK], "bfloat16"),
    "ys": ("sbuf", [128, TK], "bfloat16"),
    "acc": ("psum", [128, 512], "float32"),
    "acch": ("psum", [128, 512], "float32"),
}
SEMAPHORES = ["ldh", "ld", "zs", "hm", "mm", "hr", "sent", "cp", "st", "rawarr"] + ["arr%d" % p for p in range(NP)]


def _way(topo, a, b):
    return (0 if topo.same_plane(a, b) else 2) + (0 if topo.die(a) == topo.die(b) else 1)


def _gets_inputs(topo, p, q):
    return topo.same_plane(p, q) and topo.die(p) != topo.die(q)


def _mask(topo, src, dsts):
    m = topo.mask(src, dsts[0])
    for d in dsts:
        m &= topo.mask(src, d)
    return m


def _count(mask):
    return bin(mask).count("1")


def _send(g, topo, core, mask, dsts, src, dst, remote_sem, local_sem):
    ids = []
    for d in dsts:
        rid, pid = topo.addr(d, core)
        ids.append(DstId(rid=rid, pnc=pid))
    g.remote_dma_fused(
        [RemoteDMATransfer(dst_ids=ids, dma_engine_mask=mask, remote_sem=remote_sem,
                           srcs=[src], dsts=[dst for _ in dsts], alu_op=0)],
        local_sem=local_sem)


def _layer1(g, T, S, buf):
    g.tensor.matmul(T.acch[:, 0:TK], buf[:, TK:XW], buf[:, 0:TK], True, True).then_inc(S.hm, 1)
    g.vector.wait_ge(S.zs, 1)
    g.vector.wait_ge(S.hm, 1)
    g.vector.tensor_tensor(T.hs[:], T.acch[:, 0:TK], T.zero[:], AluOpType.max).then_inc(S.hr, 1)


def rank_program(g, core, T, topo):
    rank = T.rank_of(core)
    if rank is None:
        return
    S = T.sem
    P, Q = T.cores[:NP], T.cores[NP:]
    g.vector.memset(T.zero[:], 0.0).then_inc(S.zs, 1)
    if rank < NP:
        p = rank
        g.sync.dma_start(T.xw[:, 0:HEAD], T.x[:, 0:HEAD]).then_inc(S.ldh, 16)
        g.scalar.dma_start(T.xw[:, TK:XW], T.w1[:]).then_inc(S.ld, 16)
        g.sync.dma_start(T.xw[:, HEAD:TK], T.x[:, HEAD:TK]).then_inc(S.ld, 16)

        mask = _mask(topo, core, Q)
        first = [q for q in Q if _gets_inputs(topo, core, q)]
        rest = sorted([q for q in Q if q not in first], key=lambda q: -_way(topo, core, q))

        g.wait_ge(S.ldh, 16)
        _send(g, topo, core, mask, first, T.xw[:, 0:HEAD], T.raw[:, 0:HEAD], S.rawarr, S.sent)
        g.wait_ge(S.ld, 32)
        _send(g, topo, core, mask, first, T.xw[:, HEAD:XW], T.raw[:, HEAD:XW], S.rawarr, S.sent)

        g.tensor.wait_ge(S.ldh, 16)
        g.tensor.wait_ge(S.ld, 32)
        _layer1(g, T, S, T.xw)

        g.wait_ge(S.hr, 1)
        _send(g, topo, core, mask, rest, T.hs[:], T.land[:, p * TK:(p + 1) * TK], S["arr%d" % p], S.sent)
        g.wait_ge(S.sent, 3 * _count(mask))
    else:
        g.scalar.dma_start(T.w2s[:], T.w2[:]).then_inc(S.ld, 16)
        own = [s for s in P if _gets_inputs(topo, s, core)][0]
        rest = sorted([s for s in P if s != own], key=lambda s: -_way(topo, s, core))

        g.tensor.wait_ge(S.rawarr, 2 * _count(_mask(topo, own, Q)))
        _layer1(g, T, S, T.raw)

        g.tensor.wait_ge(S.ld, 16)
        turns = [rest[0], own] + rest[1:]
        for k, s in enumerate(turns):
            p = T.rank_of(s)
            if s == own:
                g.tensor.wait_ge(S.hr, 1)
                h = T.hs[:]
            else:
                g.tensor.wait_ge(S["arr%d" % p], _count(_mask(topo, s, Q)))
                h = T.land[:, p * TK:(p + 1) * TK]
            mmi = g.tensor.matmul(T.acc[:, 0:TK], T.w2s[:, p * 128:(p + 1) * 128], h, k == 0, k == NP - 1)
        mmi.then_inc(S.mm, 1)
        g.vector.wait_ge(S.mm, 1)
        g.vector.tensor_copy(T.ys[:], T.acc[:, 0:TK]).then_inc(S.cp, 1)
        g.sync.wait_ge(S.cp, 1)
        g.sync.dma_start(T.y[:], T.ys[:]).then_inc(S.st, 16)
        g.sync.wait_ge(S.st, 16)
